import numpy as np
import ml_dtypes


def mxq(x, axis, fmt="e4m3"):
    dtype, down = {"e4m3": (ml_dtypes.float8_e4m3fn, 7), "e5m2": (ml_dtypes.float8_e5m2, 14)}[fmt]
    v = np.moveaxis(np.asarray(x, np.float32).astype(ml_dtypes.bfloat16).astype(np.float64), axis, -1)
    blocks = v.reshape(v.shape[:-1] + (-1, 32))
    amax = np.abs(blocks).max(-1, keepdims=True)
    byte = np.maximum(np.where(amax > 0, np.frexp(amax)[1] - 1 + 127, 0) - down, 1)
    scale = np.exp2(byte - 127.0)
    codes = (blocks / scale).astype(np.float32).astype(dtype).astype(np.float64)
    return np.moveaxis((codes * scale).reshape(v.shape), -1, axis)


WIDE = False


def mx_kscale(k, group=512):
    if not WIDE:
        return np.ones(k)
    levels = np.array([10, -10, 5, -5, 0])
    if group != 512:
        return np.exp2(np.random.permutation(np.resize(levels, k // group))).repeat(group)
    if k % 512:
        return np.exp2(np.random.permutation(np.resize(levels, k // 32))).repeat(32)
    a = np.empty((k // 512, 16))
    for p in range(k // 512):
        a[p, :8] = np.random.permutation(np.resize(levels, 8))
        for g in range(8):
            far = levels[np.abs(levels - a[p, g]) >= 10]
            a[p, g + 8] = far[np.random.randint(len(far))]
    return np.exp2(a.ravel()).repeat(32)


def f64(x):
    return np.asarray(x).astype(np.float64)


def silu(v):
    return v / (1.0 + np.exp(-v))


def sigmoid(v):
    return 1.0 / (1.0 + np.exp(-v))


G, D, M, O, N = 2, 256, 128, 256, 512


def setup_inputs():
    n = np.random.standard_normal
    s_d = mx_kscale(D, 0)
    s_o = mx_kscale(O, 0)
    return {
        "x": (n((G, D, N)) * s_d[:, None]).astype(np.float32),
        "w1": (n((G, D, M)) / np.sqrt(D) / s_d[:, None]).astype(np.float32),
        "w2": (n((G, D, M)) / np.sqrt(D) / s_d[:, None]).astype(np.float32),
        "w3": (n((G, D, M)) / np.sqrt(D) / s_d[:, None]).astype(np.float32),
        "b3": (0.5 * n((G, M, 1))).astype(np.float32),
        "wo": (n((G, O, M)) / np.sqrt(O) / s_o[:, None]).astype(np.float32),
        "dy": (n((G, O, N)) * s_o[:, None]).astype(np.float32),
        "dx": (n((G, D, N)) * s_d[:, None]).astype(np.float32),
        "og": (np.random.uniform(0.5, 2.0, (G, M, 1))).astype(np.float32),
        "base": (0.3 * n((G, M, N))).astype(np.float32),
    }


def reference(x, w1, w2, w3, b3, wo, dy, dx, og, base):
    w1q = mxq(f64(w1), 1, "e4m3")
    xq = mxq(f64(x), 1, "e4m3")
    z1 = w1q.transpose(0, 2, 1) @ xq
    dxq = mxq(f64(dx), 1, "e4m3")
    tz1 = w1q.transpose(0, 2, 1) @ dxq
    w2q = mxq(f64(w2), 1, "e4m3")
    z2 = w2q.transpose(0, 2, 1) @ xq
    tz2 = w2q.transpose(0, 2, 1) @ dxq
    w3q = mxq(f64(w3), 1, "e4m3")
    z3 = w3q.transpose(0, 2, 1) @ xq
    tz3 = w3q.transpose(0, 2, 1) @ dxq
    e1 = np.tanh(z1)
    e2 = silu(z2)
    gt = sigmoid(z3 + f64(b3))
    woq = mxq(f64(wo), 1, "e4m3")
    dyq = mxq(f64(dy), 1, "e4m3")
    c0 = woq.transpose(0, 2, 1) @ dyq
    dgt = c0 * (e1 - e2)
    xe1 = tz1 * (1.0 - np.square(e1))
    xe2 = tz2 * sigmoid(z2) * (1.0 + z2 * (1.0 - sigmoid(z2)))
    xgt = tz3 * gt * (1.0 - gt)
    xdgt = (xe1 - xe2) * c0
    xdz3 = (xdgt * gt + xgt * dgt) * (1.0 - gt) + xgt * (-1.0) * dgt * gt
    y = xdz3 * f64(og) + f64(base)
    return y

@@ -1,0 +1,210 @@
+from contextlib import ExitStack
+
+import concourse.mybir as mybir
+
+G, D, M, N = 2, 256, 128, 512
+
+F32 = mybir.dt.float32
+BF16 = mybir.dt.bfloat16
+U32 = mybir.dt.uint32
+U8 = mybir.dt.uint8
+FP8X4 = mybir.dt.float8_e4m3fn_x4
+ACT = mybir.ActivationFunctionType
+ALU = mybir.AluOpType
+
+P = 128
+PACK = 4
+ROWS = D // PACK
+HALF = N // 2
+RUN = 4
+
+FLOPS = 7 * 2 * G * D * M * N
+
+
+def tile_rows_hvmixture_kernel(tc, x, w1, w2, w3, b3, wo, dy, dx, og, base, out):
+    nc = tc.nc
+
+    with ExitStack() as ctx:
+        sb = ctx.enter_context(tc.tile_pool(name="sb", bufs=1))
+        ps = ctx.enter_context(tc.psum_pool(name="ps", bufs=1))
+        ctx.enter_context(tc.manual_schedule())
+
+        def load(name, src):
+            raw = sb.tile([P, PACK, src.shape[2]], F32, name=name + "_raw")
+            nc.sync.dma_start(out=raw[:], in_=src.rearrange("g (p j) c -> (g p) j c", j=PACK))
+            return raw
+
+        def load_column(name, src):
+            padded = sb.tile([P, G, 8], F32, name=name)
+            with nc.allow_non_contiguous_dma(reason="one value a partition"):
+                nc.scalar.dma_start(out=padded[:, :, 0:1], in_=src.rearrange("g m o -> m g o"))
+            return padded
+
+        def interleave(name, copy, raw, c0, c1):
+            packed = sb.tile([P, c1 - c0, PACK], BF16, name=name, align_bytes=64)
+            copy(
+                out=packed[:].rearrange("p (c i) j -> p c j i", i=RUN),
+                in_=raw[:, :, c0:c1].rearrange("p j (c i) -> p c j i", i=RUN),
+            )
+            return packed
+
+        def operand(name, width):
+            codes = sb.tile([P, width], U32, name=name + "_codes", align_bytes=64)
+            scales = sb.tile([P, width], U8, name=name + "_scales", align_bytes=64)
+            return codes, scales
+
+        def quantize(dst, packed, c0):
+            c1 = c0 + packed.shape[1]
+            nc.vector.quantize_mx(
+                out=dst[0][:, c0:c1].bitcast(FP8X4),
+                scales=dst[1][:, c0:c1],
+                in_=packed[:].rearrange("p c j -> p (c j)"),
+            )
+
+        def product(bank, g, weights, moving):
+            rows = slice(g * ROWS, (g + 1) * ROWS)
+            nc.tensor.matmul_mx(
+                out=bank[:],
+                lhsT=weights[0][rows, :].bitcast(FP8X4),
+                lhsT_scale=weights[1][rows, :],
+                rhs=moving[0][rows, :].bitcast(FP8X4),
+                rhs_scale=moving[1][rows, :],
+                start=True,
+                stop=True,
+            )
+
+        def wide(name):
+            return sb.tile([P, G * N], F32, name=name)
+
+        def cols(g):
+            return slice(g * N, (g + 1) * N)
+
+        b3_col = load_column("b3_col", b3)
+        og_col = load_column("og_col", og)
+        x_raw = load("x", x)
+        w1_raw = load("w1", w1)
+        dx_raw = load("dx", dx)
+        w2_raw = load("w2", w2)
+        w3_raw = load("w3", w3)
+        wo_raw = load("wo", wo)
+        dy_raw = load("dy", dy)
+        base_sb = sb.tile([P, G, N], F32, name="base_sb")
+        nc.sync.dma_start(out=base_sb[:], in_=base.rearrange("g m n -> m g n"))
+
+        zero = sb.tile([P, 1], F32, name="zero")
+        nc.vector.memset(zero[:], 0.0)
+        zero_bias = sb.tile([P, 1], F32, name="zero_bias")
+        nc.scalar.activation(out=zero_bias[:], in_=zero[:], func=ACT.Silu)
+        half_b3 = sb.tile([P, G], F32, name="half_b3")
+        nc.gpsimd.tensor_scalar(out=half_b3[:], in0=b3_col[:, :, 0], scalar1=0.5, scalar2=0.0, op0=ALU.mult, op1=ALU.add)
+
+        banks = [[ps.tile([M, N], F32, name="bank_%d_%d" % (g, i)) for i in range(4)] for g in range(G)]
+
+        xq, dxq, dyq = operand("x", N), operand("dx", N), operand("dy", N)
+        w1q, w2q, w3q, woq = operand("w1", M), operand("w2", M), operand("w3", M), operand("wo", M)
+
+        e1, e1sq, e2, q2, r2, t3, t3sq = [wide(n) for n in ("e1", "e1sq", "e2", "q2", "r2", "t3", "t3sq")]
+        u1, diff, pp, xe2, f3, mm, nn, n2, hh, res, fin = [
+            wide(n) for n in ("u1", "diff", "pp", "xe2", "f3", "mm", "nn", "n2", "hh", "res", "fin")
+        ]
+
+        vcopy, scopy = nc.vector.tensor_copy, nc.scalar.copy
+
+        x_a = interleave("x_a", vcopy, x_raw, 0, HALF)
+        x_b = interleave("x_b", scopy, x_raw, HALF, N)
+        w1_p = interleave("w1_p", vcopy, w1_raw, 0, M)
+        quantize(xq, x_a, 0)
+        quantize(w1q, w1_p, 0)
+        quantize(xq, x_b, HALF)
+        for g in range(G):
+            product(banks[g][0], g, w1q, xq)
+        for g in range(G):
+            nc.scalar.activation(out=e1[:, cols(g)], in_=banks[g][0][:], func=ACT.Tanh)
+        nc.scalar.activation(out=e1sq[:], in_=e1[:], func=ACT.Square)
+
+        dx_a = interleave("dx_a", vcopy, dx_raw, 0, HALF)
+        w2_p = interleave("w2_p", vcopy, w2_raw, 0, M)
+        dx_b = interleave("dx_b", vcopy, dx_raw, HALF, N)
+        quantize(w2q, w2_p, 0)
+        for g in range(G):
+            product(banks[g][1], g, w2q, xq)
+        quantize(dxq, dx_a, 0)
+        quantize(dxq, dx_b, HALF)
+        for g in range(G):
+            product(banks[g][2], g, w1q, dxq)
+        w3_p = interleave("w3_p", scopy, w3_raw, 0, M)
+        quantize(w3q, w3_p, 0)
+        for g in range(G):
+            product(banks[g][3], g, w3q, xq)
+        for g in range(G):
+            product(banks[g][0], g, w2q, dxq)
+
+        for g in range(G):
+            nc.scalar.activation(out=e2[:, cols(g)], in_=banks[g][1][:], func=ACT.Silu, bias=zero_bias[:])
+            nc.scalar.activation(out=q2[:, cols(g)], in_=banks[g][1][:], func=ACT.Tanh, scale=0.5)
+        for g in range(G):
+            nc.vector.scalar_tensor_tensor(
+                out=u1[:, cols(g)], in0=e1sq[:, cols(g)], scalar=1.0, in1=banks[g][2][:], op0=ALU.subtract, op1=ALU.mult
+            )
+        for g in range(G):
+            product(banks[g][2], g, w3q, dxq)
+        for g in range(G):
+            nc.scalar.activation(
+                out=t3[:, cols(g)], in_=banks[g][3][:], func=ACT.Tanh, scale=0.5, bias=half_b3[:, g : g + 1]
+            )
+        nc.scalar.activation(out=t3sq[:], in_=t3[:], func=ACT.Square, scale=0.5)
+        wo_p = interleave("wo_p", scopy, wo_raw, 0, M)
+        dy_a = interleave("dy_a", scopy, dy_raw, 0, HALF)
+        dy_b = interleave("dy_b", scopy, dy_raw, HALF, N)
+
+        for g in range(G):
+            nc.vector.tensor_tensor(out=diff[:, cols(g)], in0=e1[:, cols(g)], in1=e2[:, cols(g)], op=ALU.subtract)
+            nc.vector.tensor_scalar(
+                out=r2[:, cols(g)], in0=q2[:, cols(g)], scalar1=-0.5, scalar2=0.5, op0=ALU.mult, op1=ALU.add
+            )
+        for g in range(G):
+            nc.vector.scalar_tensor_tensor(
+                out=pp[:, cols(g)], in0=e2[:, cols(g)], scalar=1.0, in1=r2[:, cols(g)], op0=ALU.subtract, op1=ALU.mult
+            )
+        for g in range(G):
+            nc.vector.scalar_tensor_tensor(
+                out=xe2[:, cols(g)], in0=pp[:, cols(g)], scalar=1.0, in1=banks[g][0][:], op0=ALU.add, op1=ALU.mult
+            )
+        for g in range(G):
+            nc.vector.tensor_tensor(out=f3[:, cols(g)], in0=diff[:, cols(g)], in1=t3[:, cols(g)], op=ALU.mult)
+        for g in range(G):
+            nc.vector.tensor_tensor(out=mm[:, cols(g)], in0=f3[:, cols(g)], in1=banks[g][2][:], op=ALU.mult)
+        quantize(woq, wo_p, 0)
+        quantize(dyq, dy_a, 0)
+        for g in range(G):
+            nc.vector.tensor_tensor(out=nn[:, cols(g)], in0=u1[:, cols(g)], in1=xe2[:, cols(g)], op=ALU.add)
+        quantize(dyq, dy_b, HALF)
+        for g in range(G):
+            product(banks[g][1], g, woq, dyq)
+        for g in range(G):
+            nc.vector.tensor_tensor(out=n2[:, cols(g)], in0=nn[:, cols(g)], in1=mm[:, cols(g)], op=ALU.add)
+
+        def gate_slope(g):
+            nc.vector.scalar_tensor_tensor(
+                out=hh[:, cols(g)], in0=t3sq[:, cols(g)], scalar=0.25, in1=banks[g][1][:], op0=ALU.subtract, op1=ALU.mult
+            )
+
+        def scale(g, c0, c1):
+            span = slice(g * N + c0, g * N + c1)
+            nc.vector.scalar_tensor_tensor(
+                out=res[:, span], in0=n2[:, span], scalar=og_col[:, g, 0:1], in1=hh[:, span], op0=ALU.mult, op1=ALU.mult
+            )
+
+        def finish(g, c0, c1):
+            span = slice(g * N + c0, g * N + c1)
+            nc.vector.tensor_tensor(out=fin[:, span], in0=res[:, span], in1=base_sb[:, g, c0:c1], op=ALU.add)
+            nc.sync.dma_start(out=out[g, :, c0:c1], in_=fin[:, span])
+
+        gate_slope(0)
+        gate_slope(1)
+        scale(0, 0, N)
+        scale(1, 0, HALF)
+        finish(0, 0, N)
+        scale(1, HALF, N)
+        finish(1, 0, HALF)
+        finish(1, HALF, N)

@@ -13,10 +13,14 @@ ACT = mybir.ActivationFunctionType
 ALU = mybir.AluOpType
 
 P = 128
+QUAD = 32
 PACK = 4
 ROWS = D // PACK
 HALF = N // 2
+N_CALL = 128
 RUN = 4
+BANKS = 4
+SHARED = 5 / 8
 
 FLOPS = 7 * 2 * G * D * M * N
 
@@ -29,66 +33,31 @@ def tile_rows_hvmixture_kernel(tc, x, w1, w2, w3, b3, wo, dy, dx, og, base, out)
         ps = ctx.enter_context(tc.psum_pool(name="ps", bufs=1))
         ctx.enter_context(tc.manual_schedule())
 
+
+        rows_in = sb.tile([P, P], F32, name="rows_in", align_bytes=64)
+        nc.vector.memset(rows_in[:], 0.0)
+        for place, vec in enumerate((b3, og)):
+            nc.scalar.dma_start(
+                out=rows_in[0:P:QUAD, G * QUAD * place : G * QUAD * (place + 1)].rearrange("q (g f) -> q g f", g=G),
+                in_=vec.rearrange("g (q f) o -> q g (f o)", q=P // QUAD),
+            )
+        columns = sb.tile([P, P], F32, name="columns", align_bytes=64)
+
         def load(name, src):
             raw = sb.tile([P, PACK, src.shape[2]], F32, name=name + "_raw")
             nc.sync.dma_start(out=raw[:], in_=src.rearrange("g (p j) c -> (g p) j c", j=PACK))
             return raw
 
-        def load_column(name, src):
-            padded = sb.tile([P, G, 8], F32, name=name)
-            with nc.allow_non_contiguous_dma(reason="one value a partition"):
-                nc.scalar.dma_start(out=padded[:, :, 0:1], in_=src.rearrange("g m o -> m g o"))
-            return padded
-
-        def interleave(name, copy, raw, c0, c1):
-            packed = sb.tile([P, c1 - c0, PACK], BF16, name=name, align_bytes=64)
-            copy(
-                out=packed[:].rearrange("p (c i) j -> p c j i", i=RUN),
-                in_=raw[:, :, c0:c1].rearrange("p j (c i) -> p c j i", i=RUN),
-            )
-            return packed
-
-        def operand(name, width):
-            codes = sb.tile([P, width], U32, name=name + "_codes", align_bytes=64)
-            scales = sb.tile([P, width], U8, name=name + "_scales", align_bytes=64)
-            return codes, scales
-
-        def quantize(dst, packed, c0):
-            c1 = c0 + packed.shape[1]
-            nc.vector.quantize_mx(
-                out=dst[0][:, c0:c1].bitcast(FP8X4),
-                scales=dst[1][:, c0:c1],
-                in_=packed[:].rearrange("p c j -> p (c j)"),
-            )
-
-        def product(bank, g, weights, moving):
-            rows = slice(g * ROWS, (g + 1) * ROWS)
-            nc.tensor.matmul_mx(
-                out=bank[:],
-                lhsT=weights[0][rows, :].bitcast(FP8X4),
-                lhsT_scale=weights[1][rows, :],
-                rhs=moving[0][rows, :].bitcast(FP8X4),
-                rhs_scale=moving[1][rows, :],
-                start=True,
-                stop=True,
-            )
-
-        def wide(name):
-            return sb.tile([P, G * N], F32, name=name)
-
-        def cols(g):
-            return slice(g * N, (g + 1) * N)
-
-        b3_col = load_column("b3_col", b3)
-        og_col = load_column("og_col", og)
-        x_raw = load("x", x)
+        base_sb = sb.tile([P, G, N], F32, name="base_sb")
+        x0_raw = load("x0", x[:, :, 0:HALF])
         w1_raw = load("w1", w1)
-        dx_raw = load("dx", dx)
         w2_raw = load("w2", w2)
         w3_raw = load("w3", w3)
+        x1_raw = load("x1", x[:, :, HALF:N])
+        dx0_raw = load("dx0", dx[:, :, 0:HALF])
+        dx1_raw = load("dx1", dx[:, :, HALF:N])
         wo_raw = load("wo", wo)
         dy_raw = load("dy", dy)
-        base_sb = sb.tile([P, G, N], F32, name="base_sb")
         nc.sync.dma_start(out=base_sb[:], in_=base.rearrange("g m n -> m g n"))
 
         zero = sb.tile([P, 1], F32, name="zero")
@@ -96,115 +65,255 @@ def tile_rows_hvmixture_kernel(tc, x, w1, w2, w3, b3, wo, dy, dx, og, base, out)
         zero_bias = sb.tile([P, 1], F32, name="zero_bias")
         nc.scalar.activation(out=zero_bias[:], in_=zero[:], func=ACT.Silu)
         half_b3 = sb.tile([P, G], F32, name="half_b3")
-        nc.gpsimd.tensor_scalar(out=half_b3[:], in0=b3_col[:, :, 0], scalar1=0.5, scalar2=0.0, op0=ALU.mult, op1=ALU.add)
 
-        banks = [[ps.tile([M, N], F32, name="bank_%d_%d" % (g, i)) for i in range(4)] for g in range(G)]
 
-        xq, dxq, dyq = operand("x", N), operand("dx", N), operand("dy", N)
-        w1q, w2q, w3q, woq = operand("w1", M), operand("w2", M), operand("w3", M), operand("wo", M)
+        banks = [[ps.tile([M, N], F32, name="bank_%d_%d" % (g, b)) for b in range(BANKS)] for g in range(G)]
 
-        e1, e1sq, e2, q2, r2, t3, t3sq = [wide(n) for n in ("e1", "e1sq", "e2", "q2", "r2", "t3", "t3sq")]
-        u1, diff, pp, xe2, f3, mm, nn, n2, hh, res, fin = [
-            wide(n) for n in ("u1", "diff", "pp", "xe2", "f3", "mm", "nn", "n2", "hh", "res", "fin")
+        t3, t3_sq, bracket, sloped, scaled, result = [
+            sb.tile([P, G, N], F32, name=name) for name in ("t3", "t3_sq", "bracket", "sloped", "scaled", "result")
         ]
+        e1, e2, t2, sig_m1, diff, diff_t3, gate_term, expert_sum, factors, expert_terms = [[], [], [], [], [], [], [], [], [], []]
+        for h in range(2):
+            for name, tiles in (
+                ("e1", e1),
+                ("e2", e2),
+                ("t2", t2),
+                ("sig_m1", sig_m1),
+                ("diff", diff),
+                ("diff_t3", diff_t3),
+                ("gate_term", gate_term),
+                ("expert_sum", expert_sum),
+            ):
+                tiles.append(sb.tile([P, G, HALF], F32, name="%s_%d" % (name, h)))
+            for name, tiles in (("factors", factors), ("expert_terms", expert_terms)):
+                tiles.append(sb.tile([P, G, 2 * HALF], F32, name="%s_%d" % (name, h)))
 
-        vcopy, scopy = nc.vector.tensor_copy, nc.scalar.copy
+        def cols(h):
+            return slice(h * HALF, (h + 1) * HALF)
 
-        x_a = interleave("x_a", vcopy, x_raw, 0, HALF)
-        x_b = interleave("x_b", scopy, x_raw, HALF, N)
-        w1_p = interleave("w1_p", vcopy, w1_raw, 0, M)
-        quantize(xq, x_a, 0)
-        quantize(w1q, w1_p, 0)
-        quantize(xq, x_b, HALF)
-        for g in range(G):
-            product(banks[g][0], g, w1q, xq)
-        for g in range(G):
-            nc.scalar.activation(out=e1[:, cols(g)], in_=banks[g][0][:], func=ACT.Tanh)
-        nc.scalar.activation(out=e1sq[:], in_=e1[:], func=ACT.Square)
+        both = slice(0, G)
 
-        dx_a = interleave("dx_a", vcopy, dx_raw, 0, HALF)
-        w2_p = interleave("w2_p", vcopy, w2_raw, 0, M)
-        dx_b = interleave("dx_b", vcopy, dx_raw, HALF, N)
-        quantize(w2q, w2_p, 0)
-        for g in range(G):
-            product(banks[g][1], g, w2q, xq)
-        quantize(dxq, dx_a, 0)
-        quantize(dxq, dx_b, HALF)
-        for g in range(G):
-            product(banks[g][2], g, w1q, dxq)
-        w3_p = interleave("w3_p", scopy, w3_raw, 0, M)
-        quantize(w3q, w3_p, 0)
-        for g in range(G):
-            product(banks[g][3], g, w3q, xq)
-        for g in range(G):
-            product(banks[g][0], g, w2q, dxq)
+        def one(g):
+            return slice(g, g + 1)
 
-        for g in range(G):
-            nc.scalar.activation(out=e2[:, cols(g)], in_=banks[g][1][:], func=ACT.Silu, bias=zero_bias[:])
-            nc.scalar.activation(out=q2[:, cols(g)], in_=banks[g][1][:], func=ACT.Tanh, scale=0.5)
-        for g in range(G):
-            nc.vector.scalar_tensor_tensor(
-                out=u1[:, cols(g)], in0=e1sq[:, cols(g)], scalar=1.0, in1=banks[g][2][:], op0=ALU.subtract, op1=ALU.mult
-            )
-        for g in range(G):
-            product(banks[g][2], g, w3q, dxq)
-        for g in range(G):
+
+        def cast(name, raw, vector_part):
+            width = raw.shape[2]
+            cut = int(width * vector_part)
+            packed = sb.tile([P, width, PACK], BF16, name=name, align_bytes=64)
+            for copy, c0, c1 in ((nc.vector.tensor_copy, 0, cut), (nc.scalar.copy, cut, width)):
+                if c1 > c0:
+                    copy(
+                        out=packed[:, c0:c1, :].rearrange("p (c i) j -> p c j i", i=RUN),
+                        in_=raw[:, :, c0:c1].rearrange("p j (c i) -> p c j i", i=RUN),
+                    )
+            return packed
+
+        def operand(name, width):
+            codes = sb.tile([P, width], U32, name=name + "_codes", align_bytes=64)
+            scales = sb.tile([P, width], U8, name=name + "_scales", align_bytes=64)
+            return codes[:], scales[:]
+
+        def quantize_into(target, packed):
+            codes, scales = target
+            nc.vector.quantize_mx(out=codes.bitcast(FP8X4), scales=scales, in_=packed[:].rearrange("p c j -> p (c j)"))
+
+        def quantize(name, packed):
+            target = operand(name, packed.shape[1])
+            quantize_into(target, packed)
+            return target
+
+        def product(g, weights, moving, bank, at):
+            rows = slice(g * ROWS, (g + 1) * ROWS)
+            for c in range(0, HALF, N_CALL):
+                nc.tensor.matmul_mx(
+                    out=banks[g][bank][:, at + c : at + c + N_CALL],
+                    lhsT=weights[0][rows, :].bitcast(FP8X4),
+                    lhsT_scale=weights[1][rows, :],
+                    rhs=moving[0][rows, c : c + N_CALL].bitcast(FP8X4),
+                    rhs_scale=moving[1][rows, c : c + N_CALL],
+                    start=True,
+                    stop=True,
+                )
+
+        def products(moving, bank, parts):
+            for g in range(G):
+                for weights, at in parts:
+                    product(g, weights, moving, bank, at)
+
+        def sums(g, bank, at, width=HALF):
+            return banks[g][bank][:, at : at + width]
+
+
+        def make_e1(h, g, bank, at):
+            nc.scalar.activation(out=e1[h][:, g, :], in_=sums(g, bank, at), func=ACT.Tanh)
+
+        def make_e2(h, g, bank, at):
+            nc.scalar.activation(out=e2[h][:, g, :], in_=sums(g, bank, at), func=ACT.Silu, bias=zero_bias[:])
+
+        def make_t2(h, g, bank, at):
+            nc.scalar.activation(out=t2[h][:, g, :], in_=sums(g, bank, at), func=ACT.Tanh, scale=0.5)
+
+        def make_t3(h, g):
             nc.scalar.activation(
-                out=t3[:, cols(g)], in_=banks[g][3][:], func=ACT.Tanh, scale=0.5, bias=half_b3[:, g : g + 1]
+                out=t3[:, g, cols(h)], in_=sums(g, 2, 0), func=ACT.Tanh, scale=0.5, bias=half_b3[:, g : g + 1]
             )
-        nc.scalar.activation(out=t3sq[:], in_=t3[:], func=ACT.Square, scale=0.5)
-        wo_p = interleave("wo_p", scopy, wo_raw, 0, M)
-        dy_a = interleave("dy_a", scopy, dy_raw, 0, HALF)
-        dy_b = interleave("dy_b", scopy, dy_raw, HALF, N)
 
-        for g in range(G):
-            nc.vector.tensor_tensor(out=diff[:, cols(g)], in0=e1[:, cols(g)], in1=e2[:, cols(g)], op=ALU.subtract)
-            nc.vector.tensor_scalar(
-                out=r2[:, cols(g)], in0=q2[:, cols(g)], scalar1=-0.5, scalar2=0.5, op0=ALU.mult, op1=ALU.add
-            )
-        for g in range(G):
+        def square_e1(h):
+            nc.scalar.activation(out=factors[h][:, :, 0:HALF], in_=e1[h][:], func=ACT.Square)
+
+        def square_t3(h):
+            nc.scalar.activation(out=t3_sq[:, :, cols(h)], in_=t3[:, :, cols(h)], func=ACT.Square, scale=0.5)
+
+
+        def make_diff(h, gs):
+            nc.vector.tensor_tensor(out=diff[h][:, gs, :], in0=e1[h][:, gs, :], in1=e2[h][:, gs, :], op=ALU.subtract)
+
+        def make_silu_factor(h):
             nc.vector.scalar_tensor_tensor(
-                out=pp[:, cols(g)], in0=e2[:, cols(g)], scalar=1.0, in1=r2[:, cols(g)], op0=ALU.subtract, op1=ALU.mult
+                out=factors[h][:, :, HALF:], in0=e2[h][:], scalar=1.0, in1=sig_m1[h][:], op0=ALU.subtract, op1=ALU.mult
             )
-        for g in range(G):
+
+        def make_diff_t3(h):
+            nc.vector.tensor_tensor(out=diff_t3[h][:], in0=diff[h][:], in1=t3[:, :, cols(h)], op=ALU.mult)
+
+        def make_expert_terms(h, g, bank):
             nc.vector.scalar_tensor_tensor(
-                out=xe2[:, cols(g)], in0=pp[:, cols(g)], scalar=1.0, in1=banks[g][0][:], op0=ALU.add, op1=ALU.mult
+                out=expert_terms[h][:, g, :],
+                in0=factors[h][:, g, :],
+                scalar=1.0,
+                in1=sums(g, bank, 0, 2 * HALF),
+                op0=ALU.subtract,
+                op1=ALU.mult,
             )
-        for g in range(G):
-            nc.vector.tensor_tensor(out=f3[:, cols(g)], in0=diff[:, cols(g)], in1=t3[:, cols(g)], op=ALU.mult)
-        for g in range(G):
-            nc.vector.tensor_tensor(out=mm[:, cols(g)], in0=f3[:, cols(g)], in1=banks[g][2][:], op=ALU.mult)
-        quantize(woq, wo_p, 0)
-        quantize(dyq, dy_a, 0)
-        for g in range(G):
-            nc.vector.tensor_tensor(out=nn[:, cols(g)], in0=u1[:, cols(g)], in1=xe2[:, cols(g)], op=ALU.add)
-        quantize(dyq, dy_b, HALF)
-        for g in range(G):
-            product(banks[g][1], g, woq, dyq)
-        for g in range(G):
-            nc.vector.tensor_tensor(out=n2[:, cols(g)], in0=nn[:, cols(g)], in1=mm[:, cols(g)], op=ALU.add)
 
-        def gate_slope(g):
+        def make_gate_term(h, g, bank):
+            nc.vector.tensor_tensor(out=gate_term[h][:, g, :], in0=diff_t3[h][:, g, :], in1=sums(g, bank, 0), op=ALU.mult)
+
+        def make_expert_sum(engine, h, gs):
+            engine.tensor_tensor(
+                out=expert_sum[h][:, gs, :],
+                in0=expert_terms[h][:, gs, 0:HALF],
+                in1=expert_terms[h][:, gs, HALF:],
+                op=ALU.subtract,
+            )
+
+        def make_bracket(engine, h):
+            engine.tensor_tensor(out=bracket[:, :, cols(h)], in0=expert_sum[h][:], in1=gate_term[h][:], op=ALU.add)
+
+        def make_sloped(h):
             nc.vector.scalar_tensor_tensor(
-                out=hh[:, cols(g)], in0=t3sq[:, cols(g)], scalar=0.25, in1=banks[g][1][:], op0=ALU.subtract, op1=ALU.mult
+                out=sloped[:, :, cols(h)],
+                in0=t3_sq[:, :, cols(h)],
+                scalar=0.25,
+                in1=bracket[:, :, cols(h)],
+                op0=ALU.subtract,
+                op1=ALU.mult,
             )
 
-        def scale(g, c0, c1):
-            span = slice(g * N + c0, g * N + c1)
+        def make_scaled(h, g):
+            og_at = QUAD * (G + g)
             nc.vector.scalar_tensor_tensor(
-                out=res[:, span], in0=n2[:, span], scalar=og_col[:, g, 0:1], in1=hh[:, span], op0=ALU.mult, op1=ALU.mult
+                out=scaled[:, g, cols(h)],
+                in0=sums(g, h, h * HALF),
+                scalar=columns[:, og_at : og_at + 1],
+                in1=sloped[:, g, cols(h)],
+                op0=ALU.mult,
+                op1=ALU.mult,
             )
 
-        def finish(g, c0, c1):
-            span = slice(g * N + c0, g * N + c1)
-            nc.vector.tensor_tensor(out=fin[:, span], in0=res[:, span], in1=base_sb[:, g, c0:c1], op=ALU.add)
-            nc.sync.dma_start(out=out[g, :, c0:c1], in_=fin[:, span])
+        def finish(h, gs, queue):
+            nc.vector.tensor_tensor(
+                out=result[:, gs, cols(h)], in0=scaled[:, gs, cols(h)], in1=base_sb[:, gs, cols(h)], op=ALU.add
+            )
+            queue.dma_start(out=out[gs, :, cols(h)].rearrange("g m n -> m g n"), in_=result[:, gs, cols(h)])
 
-        gate_slope(0)
-        gate_slope(1)
-        scale(0, 0, N)
-        scale(1, 0, HALF)
-        finish(0, 0, N)
-        scale(1, HALF, N)
-        finish(1, 0, HALF)
-        finish(1, HALF, N)
+
+        x0_bf = cast("x0_bf", x0_raw, SHARED)
+        w1_bf = cast("w1_bf", w1_raw, SHARED)
+        x0_q = quantize("x0", x0_bf)
+        w1_q = quantize("w1", w1_bf)
+        products(x0_q, 0, [(w1_q, 0)])
+        w2_q = quantize("w2", cast("w2_bf", w2_raw, SHARED))
+        products(x0_q, 1, [(w2_q, 0)])
+        for g in range(G):
+            make_e1(0, g, 0, 0)
+        w3_bf = cast("w3_bf", w3_raw, 1)
+        nc.vector.transpose(out=columns[:], in_=rows_in[:])
+        w3_q = quantize("w3", w3_bf)
+        products(x0_q, 2, [(w3_q, 0)])
+        nc.vector.tensor_scalar(out=half_b3[:], in0=columns[:, 0 : G * QUAD : QUAD], scalar1=0.5, scalar2=None, op0=ALU.mult)
+        for g in range(G):
+            make_e2(0, g, 1, 0)
+            make_t2(0, g, 1, 0)
+        make_t3(0, 0)
+
+        x1_bf = cast("x1_bf", x1_raw, 1)
+        make_diff(0, one(0))
+        x1_q = quantize("x1", x1_bf)
+        products(x1_q, 3, [(w2_q, HALF), (w1_q, 0)])
+        make_diff(0, one(1))
+        dx0_bf = cast("dx0_bf", dx0_raw, SHARED)
+        make_t3(0, 1)
+        nc.vector.tensor_scalar(out=sig_m1[0][:], in0=t2[0][:], scalar1=0.5, scalar2=-0.5, op0=ALU.mult, op1=ALU.add)
+        square_e1(0)
+        dx0_q = quantize("dx0", dx0_bf)
+        products(dx0_q, 0, [(w1_q, 0), (w2_q, HALF)])
+        products(dx0_q, 1, [(w3_q, 0)])
+        products(x1_q, 2, [(w3_q, 0)])
+        make_silu_factor(0)
+
+        for g in range(G):
+            make_e2(1, g, 3, HALF)
+            make_e1(1, g, 3, 0)
+            make_t2(1, g, 3, HALF)
+        dx1_bf = cast("dx1_bf", dx1_raw, 0)
+        for g in range(G):
+            make_t3(1, g)
+        nc.scalar.activation(out=sig_m1[1][:], in_=t2[1][:], func=ACT.Copy, scale=0.5, bias=-0.5)
+        square_e1(1)
+
+        make_diff_t3(0)
+        make_expert_terms(0, 0, 0)
+        make_expert_sum(nc.gpsimd, 0, one(0))
+        make_expert_terms(0, 1, 0)
+        for g in range(G):
+            make_gate_term(0, g, 1)
+        make_diff(1, both)
+        dx1_q = quantize("dx1", dx1_bf)
+        products(dx1_q, 3, [(w1_q, 0), (w2_q, HALF)])
+        products(dx1_q, 2, [(w3_q, 0)])
+        make_diff_t3(1)
+        make_silu_factor(1)
+        make_expert_sum(nc.vector, 0, one(1))
+        make_bracket(nc.gpsimd, 0)
+
+        wo_bf = cast("wo_bf", wo_raw, 0)
+        dy0_bf = cast("dy0_bf", dy_raw[:, :, cols(0)], 0)
+        square_t3(0)
+        dy1_bf = cast("dy1_bf", dy_raw[:, :, cols(1)], 0)
+        square_t3(1)
+
+        for g in range(G):
+            make_expert_terms(1, g, 3)
+        for g in range(G):
+            make_gate_term(1, g, 2)
+        wo_q = quantize("wo", wo_bf)
+        dy_codes, dy_scales = operand("dy", N)
+        dy_q = [(dy_codes[:, cols(h)], dy_scales[:, cols(h)]) for h in range(2)]
+        quantize_into(dy_q[0], dy0_bf)
+        products(dy_q[0], 0, [(wo_q, 0)])
+        make_expert_sum(nc.vector, 1, both)
+        make_sloped(0)
+        make_bracket(nc.vector, 1)
+        quantize_into(dy_q[1], dy1_bf)
+        products(dy_q[1], 1, [(wo_q, HALF)])
+
+        for g in range(G):
+            make_scaled(0, g)
+        make_sloped(1)
+        finish(0, both, nc.sync)
+        for g in range(G):
+            make_scaled(1, g)
+        finish(1, one(0), nc.sync)
+        finish(1, one(1), nc.scalar)

from contextlib import ExitStack

import concourse.mybir as mybir

G, D, M, N = 2, 256, 128, 512

F32 = mybir.dt.float32
BF16 = mybir.dt.bfloat16
U32 = mybir.dt.uint32
U8 = mybir.dt.uint8
FP8X4 = mybir.dt.float8_e4m3fn_x4
ACT = mybir.ActivationFunctionType
ALU = mybir.AluOpType

P = 128
QUAD = 32
PACK = 4
ROWS = D // PACK
HALF = N // 2
N_CALL = 128
RUN = 4
BANKS = 4
SHARED = 5 / 8

FLOPS = 7 * 2 * G * D * M * N


def tile_rows_hvmixture_kernel(tc, x, w1, w2, w3, b3, wo, dy, dx, og, base, out):
    nc = tc.nc

    with ExitStack() as ctx:
        sb = ctx.enter_context(tc.tile_pool(name="sb", bufs=1))
        ps = ctx.enter_context(tc.psum_pool(name="ps", bufs=1))
        ctx.enter_context(tc.manual_schedule())


        rows_in = sb.tile([P, P], F32, name="rows_in", align_bytes=64)
        nc.vector.memset(rows_in[:], 0.0)
        for place, vec in enumerate((b3, og)):
            nc.scalar.dma_start(
                out=rows_in[0:P:QUAD, G * QUAD * place : G * QUAD * (place + 1)].rearrange("q (g f) -> q g f", g=G),
                in_=vec.rearrange("g (q f) o -> q g (f o)", q=P // QUAD),
            )
        columns = sb.tile([P, P], F32, name="columns", align_bytes=64)

        def load(name, src):
            raw = sb.tile([P, PACK, src.shape[2]], F32, name=name + "_raw")
            nc.sync.dma_start(out=raw[:], in_=src.rearrange("g (p j) c -> (g p) j c", j=PACK))
            return raw

        base_sb = sb.tile([P, G, N], F32, name="base_sb")
        x0_raw = load("x0", x[:, :, 0:HALF])
        w1_raw = load("w1", w1)
        w2_raw = load("w2", w2)
        w3_raw = load("w3", w3)
        x1_raw = load("x1", x[:, :, HALF:N])
        dx0_raw = load("dx0", dx[:, :, 0:HALF])
        dx1_raw = load("dx1", dx[:, :, HALF:N])
        wo_raw = load("wo", wo)
        dy_raw = load("dy", dy)
        nc.sync.dma_start(out=base_sb[:], in_=base.rearrange("g m n -> m g n"))

        zero = sb.tile([P, 1], F32, name="zero")
        nc.vector.memset(zero[:], 0.0)
        zero_bias = sb.tile([P, 1], F32, name="zero_bias")
        nc.scalar.activation(out=zero_bias[:], in_=zero[:], func=ACT.Silu)
        half_b3 = sb.tile([P, G], F32, name="half_b3")


        banks = [[ps.tile([M, N], F32, name="bank_%d_%d" % (g, b)) for b in range(BANKS)] for g in range(G)]

        t3, t3_sq, bracket, sloped, scaled, result = [
            sb.tile([P, G, N], F32, name=name) for name in ("t3", "t3_sq", "bracket", "sloped", "scaled", "result")
        ]
        e1, e2, t2, sig_m1, diff, diff_t3, gate_term, expert_sum, factors, expert_terms = [[], [], [], [], [], [], [], [], [], []]
        for h in range(2):
            for name, tiles in (
                ("e1", e1),
                ("e2", e2),
                ("t2", t2),
                ("sig_m1", sig_m1),
                ("diff", diff),
                ("diff_t3", diff_t3),
                ("gate_term", gate_term),
                ("expert_sum", expert_sum),
            ):
                tiles.append(sb.tile([P, G, HALF], F32, name="%s_%d" % (name, h)))
            for name, tiles in (("factors", factors), ("expert_terms", expert_terms)):
                tiles.append(sb.tile([P, G, 2 * HALF], F32, name="%s_%d" % (name, h)))

        def cols(h):
            return slice(h * HALF, (h + 1) * HALF)

        both = slice(0, G)

        def one(g):
            return slice(g, g + 1)


        def cast(name, raw, vector_part):
            width = raw.shape[2]
            cut = int(width * vector_part)
            packed = sb.tile([P, width, PACK], BF16, name=name, align_bytes=64)
            for copy, c0, c1 in ((nc.vector.tensor_copy, 0, cut), (nc.scalar.copy, cut, width)):
                if c1 > c0:
                    copy(
                        out=packed[:, c0:c1, :].rearrange("p (c i) j -> p c j i", i=RUN),
                        in_=raw[:, :, c0:c1].rearrange("p j (c i) -> p c j i", i=RUN),
                    )
            return packed

        def operand(name, width):
            codes = sb.tile([P, width], U32, name=name + "_codes", align_bytes=64)
            scales = sb.tile([P, width], U8, name=name + "_scales", align_bytes=64)
            return codes[:], scales[:]

        def quantize_into(target, packed):
            codes, scales = target
            nc.vector.quantize_mx(out=codes.bitcast(FP8X4), scales=scales, in_=packed[:].rearrange("p c j -> p (c j)"))

        def quantize(name, packed):
            target = operand(name, packed.shape[1])
            quantize_into(target, packed)
            return target

        def product(g, weights, moving, bank, at):
            rows = slice(g * ROWS, (g + 1) * ROWS)
            for c in range(0, HALF, N_CALL):
                nc.tensor.matmul_mx(
                    out=banks[g][bank][:, at + c : at + c + N_CALL],
                    lhsT=weights[0][rows, :].bitcast(FP8X4),
                    lhsT_scale=weights[1][rows, :],
                    rhs=moving[0][rows, c : c + N_CALL].bitcast(FP8X4),
                    rhs_scale=moving[1][rows, c : c + N_CALL],
                    start=True,
                    stop=True,
                )

        def products(moving, bank, parts):
            for g in range(G):
                for weights, at in parts:
                    product(g, weights, moving, bank, at)

        def sums(g, bank, at, width=HALF):
            return banks[g][bank][:, at : at + width]


        def make_e1(h, g, bank, at):
            nc.scalar.activation(out=e1[h][:, g, :], in_=sums(g, bank, at), func=ACT.Tanh)

        def make_e2(h, g, bank, at):
            nc.scalar.activation(out=e2[h][:, g, :], in_=sums(g, bank, at), func=ACT.Silu, bias=zero_bias[:])

        def make_t2(h, g, bank, at):
            nc.scalar.activation(out=t2[h][:, g, :], in_=sums(g, bank, at), func=ACT.Tanh, scale=0.5)

        def make_t3(h, g):
            nc.scalar.activation(
                out=t3[:, g, cols(h)], in_=sums(g, 2, 0), func=ACT.Tanh, scale=0.5, bias=half_b3[:, g : g + 1]
            )

        def square_e1(h):
            nc.scalar.activation(out=factors[h][:, :, 0:HALF], in_=e1[h][:], func=ACT.Square)

        def square_t3(h):
            nc.scalar.activation(out=t3_sq[:, :, cols(h)], in_=t3[:, :, cols(h)], func=ACT.Square, scale=0.5)


        def make_diff(h, gs):
            nc.vector.tensor_tensor(out=diff[h][:, gs, :], in0=e1[h][:, gs, :], in1=e2[h][:, gs, :], op=ALU.subtract)

        def make_silu_factor(h):
            nc.vector.scalar_tensor_tensor(
                out=factors[h][:, :, HALF:], in0=e2[h][:], scalar=1.0, in1=sig_m1[h][:], op0=ALU.subtract, op1=ALU.mult
            )

        def make_diff_t3(h):
            nc.vector.tensor_tensor(out=diff_t3[h][:], in0=diff[h][:], in1=t3[:, :, cols(h)], op=ALU.mult)

        def make_expert_terms(h, g, bank):
            nc.vector.scalar_tensor_tensor(
                out=expert_terms[h][:, g, :],
                in0=factors[h][:, g, :],
                scalar=1.0,
                in1=sums(g, bank, 0, 2 * HALF),
                op0=ALU.subtract,
                op1=ALU.mult,
            )

        def make_gate_term(h, g, bank):
            nc.vector.tensor_tensor(out=gate_term[h][:, g, :], in0=diff_t3[h][:, g, :], in1=sums(g, bank, 0), op=ALU.mult)

        def make_expert_sum(engine, h, gs):
            engine.tensor_tensor(
                out=expert_sum[h][:, gs, :],
                in0=expert_terms[h][:, gs, 0:HALF],
                in1=expert_terms[h][:, gs, HALF:],
                op=ALU.subtract,
            )

        def make_bracket(engine, h):
            engine.tensor_tensor(out=bracket[:, :, cols(h)], in0=expert_sum[h][:], in1=gate_term[h][:], op=ALU.add)

        def make_sloped(h):
            nc.vector.scalar_tensor_tensor(
                out=sloped[:, :, cols(h)],
                in0=t3_sq[:, :, cols(h)],
                scalar=0.25,
                in1=bracket[:, :, cols(h)],
                op0=ALU.subtract,
                op1=ALU.mult,
            )

        def make_scaled(h, g):
            og_at = QUAD * (G + g)
            nc.vector.scalar_tensor_tensor(
                out=scaled[:, g, cols(h)],
                in0=sums(g, h, h * HALF),
                scalar=columns[:, og_at : og_at + 1],
                in1=sloped[:, g, cols(h)],
                op0=ALU.mult,
                op1=ALU.mult,
            )

        def finish(h, gs, queue):
            nc.vector.tensor_tensor(
                out=result[:, gs, cols(h)], in0=scaled[:, gs, cols(h)], in1=base_sb[:, gs, cols(h)], op=ALU.add
            )
            queue.dma_start(out=out[gs, :, cols(h)].rearrange("g m n -> m g n"), in_=result[:, gs, cols(h)])


        x0_bf = cast("x0_bf", x0_raw, SHARED)
        w1_bf = cast("w1_bf", w1_raw, SHARED)
        x0_q = quantize("x0", x0_bf)
        w1_q = quantize("w1", w1_bf)
        products(x0_q, 0, [(w1_q, 0)])
        w2_q = quantize("w2", cast("w2_bf", w2_raw, SHARED))
        products(x0_q, 1, [(w2_q, 0)])
        for g in range(G):
            make_e1(0, g, 0, 0)
        w3_bf = cast("w3_bf", w3_raw, 1)
        nc.vector.transpose(out=columns[:], in_=rows_in[:])
        w3_q = quantize("w3", w3_bf)
        products(x0_q, 2, [(w3_q, 0)])
        nc.vector.tensor_scalar(out=half_b3[:], in0=columns[:, 0 : G * QUAD : QUAD], scalar1=0.5, scalar2=None, op0=ALU.mult)
        for g in range(G):
            make_e2(0, g, 1, 0)
            make_t2(0, g, 1, 0)
        make_t3(0, 0)

        x1_bf = cast("x1_bf", x1_raw, 1)
        make_diff(0, one(0))
        x1_q = quantize("x1", x1_bf)
        products(x1_q, 3, [(w2_q, HALF), (w1_q, 0)])
        make_diff(0, one(1))
        dx0_bf = cast("dx0_bf", dx0_raw, SHARED)
        make_t3(0, 1)
        nc.vector.tensor_scalar(out=sig_m1[0][:], in0=t2[0][:], scalar1=0.5, scalar2=-0.5, op0=ALU.mult, op1=ALU.add)
        square_e1(0)
        dx0_q = quantize("dx0", dx0_bf)
        products(dx0_q, 0, [(w1_q, 0), (w2_q, HALF)])
        products(dx0_q, 1, [(w3_q, 0)])
        products(x1_q, 2, [(w3_q, 0)])
        make_silu_factor(0)

        for g in range(G):
            make_e2(1, g, 3, HALF)
            make_e1(1, g, 3, 0)
            make_t2(1, g, 3, HALF)
        dx1_bf = cast("dx1_bf", dx1_raw, 0)
        for g in range(G):
            make_t3(1, g)
        nc.scalar.activation(out=sig_m1[1][:], in_=t2[1][:], func=ACT.Copy, scale=0.5, bias=-0.5)
        square_e1(1)

        make_diff_t3(0)
        make_expert_terms(0, 0, 0)
        make_expert_sum(nc.gpsimd, 0, one(0))
        make_expert_terms(0, 1, 0)
        for g in range(G):
            make_gate_term(0, g, 1)
        make_diff(1, both)
        dx1_q = quantize("dx1", dx1_bf)
        products(dx1_q, 3, [(w1_q, 0), (w2_q, HALF)])
        products(dx1_q, 2, [(w3_q, 0)])
        make_diff_t3(1)
        make_silu_factor(1)
        make_expert_sum(nc.vector, 0, one(1))
        make_bracket(nc.gpsimd, 0)

        wo_bf = cast("wo_bf", wo_raw, 0)
        dy0_bf = cast("dy0_bf", dy_raw[:, :, cols(0)], 0)
        square_t3(0)
        dy1_bf = cast("dy1_bf", dy_raw[:, :, cols(1)], 0)
        square_t3(1)

        for g in range(G):
            make_expert_terms(1, g, 3)
        for g in range(G):
            make_gate_term(1, g, 2)
        wo_q = quantize("wo", wo_bf)
        dy_codes, dy_scales = operand("dy", N)
        dy_q = [(dy_codes[:, cols(h)], dy_scales[:, cols(h)]) for h in range(2)]
        quantize_into(dy_q[0], dy0_bf)
        products(dy_q[0], 0, [(wo_q, 0)])
        make_expert_sum(nc.vector, 1, both)
        make_sloped(0)
        make_bracket(nc.vector, 1)
        quantize_into(dy_q[1], dy1_bf)
        products(dy_q[1], 1, [(wo_q, HALF)])

        for g in range(G):
            make_scaled(0, g)
        make_sloped(1)
        finish(0, both, nc.sync)
        for g in range(G):
            make_scaled(1, g)
        finish(1, one(0), nc.sync)
        finish(1, one(1), nc.scalar)
